import numpy as np
import ml_dtypes


def mxq(x, axis, fmt="e4m3"):
    dtype, down = {"e4m3": (ml_dtypes.float8_e4m3fn, 7), "e5m2": (ml_dtypes.float8_e5m2, 14)}[fmt]
    v = np.moveaxis(np.asarray(x, np.float32).astype(ml_dtypes.bfloat16).astype(np.float64), axis, -1)
    blocks = v.reshape(v.shape[:-1] + (-1, 32))
    amax = np.abs(blocks).max(-1, keepdims=True)
    byte = np.maximum(np.where(amax > 0, np.frexp(amax)[1] - 1 + 127, 0) - down, 1)
    scale = np.exp2(byte - 127.0)
    codes = (blocks / scale).astype(np.float32).astype(dtype).astype(np.float64)
    return np.moveaxis((codes * scale).reshape(v.shape), -1, axis)


WIDE = False


def mx_kscale(k):
    if not WIDE:
        return np.ones(k)
    levels = np.array([10, -10, 5, -5, 0])
    if k % 512:
        return np.exp2(np.random.permutation(np.resize(levels, k // 32))).repeat(32)
    a = np.empty((k // 512, 16))
    for p in range(k // 512):
        a[p, :8] = np.random.permutation(np.resize(levels, 8))
        for g in range(8):
            far = levels[np.abs(levels - a[p, g]) >= 10]
            a[p, g + 8] = far[np.random.randint(len(far))]
    return np.exp2(a.ravel()).repeat(32)


BF16 = ml_dtypes.bfloat16


def bf(x):
    return np.asarray(x, np.float32).astype(BF16)


def f64(x):
    return np.asarray(x).astype(np.float64)

def planes(Y):
    n, m = Y.shape
    b = f64(bf(Y)).reshape(n // 32, 32, m)
    amax = np.abs(b).max(1)
    byte = np.clip(np.where(amax > 0, np.frexp(amax)[1] - 1 + 127 - 7, 1), 1, 254)
    codes = (b * np.exp2(127.0 - byte)[:, None, :]).reshape(n, m).astype(np.float32).astype(ml_dtypes.float8_e4m3fn).view(np.uint8)
    words = codes.reshape(n // 512, 128, 4, m).transpose(0, 1, 3, 2)
    return np.ascontiguousarray(words), np.ascontiguousarray(byte.astype(np.uint8).reshape(n // 512, 16, m))


M, N, R = 1024, 2048, 512


def _pos(t):
    return np.maximum(t, 0.0)


def _neg(t):
    return np.maximum(-t, 0.0)


def setup_inputs():
    u = mx_kscale(M)
    t = mx_kscale(R)
    return {
        "x": bf(np.random.standard_normal((M, N)) * u[:, None]),
        "f": bf(np.random.standard_normal((M, R)) / np.sqrt(M) * u[:, None]),
        "w": bf(np.random.uniform(0.5, 1.5, M) / (u * u)),
        "g": bf(np.random.uniform(0.2, 1.8, (N, R))),
        "p": bf(np.random.standard_normal(R) * t),
        "q": bf((1.0 + 0.2 * np.random.standard_normal(R)) / t),
    }


def core(x, f, w, g, p, q):
    x, f, w, g, p, q = f64(x), f64(f), f64(w), f64(g), f64(p), f64(q)
    fw = mxq(w[:, None] * f, 0, "e4m3")
    a = mxq(x, 0, "e4m3").T @ fw
    b = q[:, None] * (mxq(f, 0, "e4m3").T @ fw)
    c = mxq(g * p[None, :], 1, "e4m3") @ mxq(b, 0, "e4m3")
    s = np.where(p >= 0, 1.0, -1.0)
    sa = a * s[None, :]
    sc = c * s[None, :]
    num = _pos(sa) + _neg(sc) + 0.5
    den = _neg(sa) + _pos(sc) + 0.5
    return g * np.sqrt(num / den)


def reference(x, f, w, g, p, q):
    R_out = core(x, f, w, g, p, q)
    words, scales = planes(R_out)
    return R_out, words, scales

@@ -1,0 +1,342 @@
+from contextlib import ExitStack
+
+import concourse.mybir as mybir
+from concourse.masks import make_identity
+
+M, N, R = 1024, 2048, 512
+FLOPS = 2 * M * N * R + 2 * M * R * R + 2 * N * R * R
+
+F32 = mybir.dt.float32
+BF16 = mybir.dt.bfloat16
+I32 = mybir.dt.int32
+U32 = mybir.dt.uint32
+U8 = mybir.dt.uint8
+FP8X4 = mybir.dt.float8_e4m3fn_x4
+ALU = mybir.AluOpType
+ACT = mybir.ActivationFunctionType
+
+P = 128
+PACK = 4
+ROWS = P * PACK
+HALVES = M // ROWS
+GROUPS = N // ROWS
+OFFSET = 0.5
+
+
+def tile_weightedsignedseminmfupdate_x1_kernel(tc, x, f, w, g, p, q, out, words, scales):
+    nc = tc.nc
+    with ExitStack() as ctx:
+        keep = ctx.enter_context(tc.tile_pool(name="keep", bufs=1))
+        work = ctx.enter_context(tc.tile_pool(name="work", bufs=2))
+        psum = ctx.enter_context(tc.psum_pool(name="psum", bufs=2))
+
+        def kept(shape, dtype, name):
+            return keep.tile(shape, dtype, name=name, align_bytes=64)
+
+        def temp(shape, dtype, name, bufs=2):
+            return work.tile(shape, dtype, name=name, bufs=bufs, align_bytes=64)
+
+        p_col = kept([P, PACK], BF16, "p_col")
+        q_col = kept([P, PACK], BF16, "q_col")
+        w_col = kept([P, HALVES, PACK], BF16, "w_col")
+        f_raw = [kept([P, PACK, R], BF16, "f_raw%d" % h) for h in range(HALVES)]
+        g_raw = [kept([P, PACK, R], BF16, "g_raw%d" % i) for i in range(GROUPS)]
+        x_raw = [[kept([P, PACK, ROWS], BF16, "x_raw%d%d" % (i, h)) for h in range(HALVES)] for i in range(GROUPS)]
+
+        def load_f(h):
+            nc.sync.dma_start(out=f_raw[h][:], in_=f[h * ROWS:(h + 1) * ROWS, :].rearrange("(k j) r -> k j r", j=PACK))
+
+        def load_g(i):
+            nc.sync.dma_start(out=g_raw[i][:], in_=g[i * ROWS:(i + 1) * ROWS, :].rearrange("(m t) r -> m t r", t=PACK))
+
+        def load_x(i, h):
+            nc.sync.dma_start(
+                out=x_raw[i][h][:],
+                in_=x[h * ROWS:(h + 1) * ROWS, i * ROWS:(i + 1) * ROWS].rearrange("(k j) n -> k j n", j=PACK),
+            )
+
+        ident_b = kept([P, P], BF16, "ident_b")
+        ident_f = kept([P, P], F32, "ident_f")
+        make_identity(nc, ident_b[:])
+        make_identity(nc, ident_f[:])
+
+
+        nc.sync.dma_start(out=p_col[:], in_=p.rearrange("(k t) -> k t", t=PACK))
+        load_f(0)
+        load_f(1)
+        nc.sync.dma_start(out=w_col[:], in_=w.rearrange("(h k j) -> k h j", h=HALVES, j=PACK))
+        nc.sync.dma_start(out=q_col[:], in_=q.rearrange("(k t) -> k t", t=PACK))
+        load_x(0, 0)
+        load_x(0, 1)
+        load_g(0)
+        for i in range(1, GROUPS):
+            load_g(i)
+            load_x(i, 0)
+            load_x(i, 1)
+
+        def pair(width, name):
+            return kept([P, width], U32, name + "_codes"), kept([P, width], U8, name + "_scales")
+
+        f_q = [pair(R, "fq%d" % h) for h in range(HALVES)]
+        fw_q = [pair(R, "fwq%d" % h) for h in range(HALVES)]
+        b_q = pair(R, "bq")
+        x_q = [[pair(ROWS, "xq%d%d" % (i, h)) for h in range(HALVES)] for i in range(GROUPS)]
+        g_q = [pair(ROWS, "gq%d" % i) for i in range(GROUPS)]
+
+        def quantize(dst, cols, values):
+            nc.vector.quantize_mx(out=dst[0][:, cols].bitcast(FP8X4), scales=dst[1][:, cols], in_=values)
+
+        def multiply(acc, left, left_cols, right, right_cols, start, stop):
+            nc.tensor.matmul_mx(
+                out=acc,
+                lhsT=left[0][:, left_cols].bitcast(FP8X4),
+                lhsT_scale=left[1][:, left_cols],
+                rhs=right[0][:, right_cols].bitcast(FP8X4),
+                rhs_scale=right[1][:, right_cols],
+                start=start,
+                stop=stop,
+            )
+
+        every = slice(0, R)
+
+        def tile_cols(t):
+            return slice(t * P, (t + 1) * P)
+
+        s_bank = psum.tile([P, R], F32, name="gt", bufs=2)
+        for t in range(PACK):
+            nc.tensor.matmul(out=s_bank[:, tile_cols(t)], lhsT=p_col[:, t:t + 1].to_broadcast([P, P]), rhs=ident_b[:], start=True, stop=True)
+        s_two = kept([P, R], BF16, "s_two")
+        s_row = kept([P, R], BF16, "s_row")
+        nc.vector.tensor_scalar(out=s_two[:].rearrange("p (m t) -> p m t", t=PACK), in0=s_bank[:].rearrange("p (t m) -> p m t", t=PACK), scalar1=0.0, scalar2=2.0, op0=ALU.is_ge, op1=ALU.mult)
+        s_col = kept([P, PACK], F32, "s_col")
+        qs_col = kept([P, PACK], F32, "qs_col")
+        nc.vector.tensor_scalar(out=s_col[:], in0=p_col[:], scalar1=0.0, scalar2=2.0, op0=ALU.is_ge, op1=ALU.mult)
+        nc.vector.tensor_scalar(out=s_row[:], in0=s_two[:], scalar1=1.0, scalar2=None, op0=ALU.subtract)
+
+        fs = f_raw
+        f_il = [temp([P, R, PACK], BF16, "lay", bufs=7) for h in range(HALVES)]
+        fw_il = [temp([P, R, PACK], BF16, "lay", bufs=7) for h in range(HALVES)]
+
+        def sign_f(h):
+            nc.vector.tensor_tensor(out=fs[h][:], in0=f_raw[h][:], in1=s_row[:].unsqueeze(1).to_broadcast([P, PACK, R]), op=ALU.mult)
+
+        def interleave(engine, dst, src, ts=slice(0, PACK)):
+            o = dst[:].rearrange("p (t m) j -> p t m j", t=PACK)[:, ts, :, :]
+            i = src[:].rearrange("p j (m t) -> p t m j", t=PACK)[:, ts, :, :]
+            if engine == "V":
+                nc.vector.tensor_copy(out=o, in_=i)
+            else:
+                nc.scalar.copy(out=o, in_=i)
+
+        def weigh_f(h):
+            nc.vector.tensor_tensor(out=fw_il[h][:], in0=f_il[h][:], in1=w_col[:, h, :].unsqueeze(1).to_broadcast([P, R, PACK]), op=ALU.mult)
+
+        def flat(t):
+            return t[:].rearrange("p c j -> p (c j)")
+
+        def gram(c):
+            bank = psum.tile([P, PACK, P], F32, name=("a_bank", "c_bank")[c % 2], bufs=3)
+            for t in range(PACK):
+                for h in range(HALVES):
+                    multiply(bank[:, t, :], f_q[h], tile_cols(t), fw_q[h], tile_cols(c), h == 0, h == HALVES - 1)
+            return bank
+
+        b_il = temp([P, R, PACK], BF16, "lay", bufs=7)
+
+        def gain_b(c, bank):
+            nc.vector.tensor_tensor(out=b_il[:, tile_cols(c), :], in0=bank[:].rearrange("p t r -> p r t"), in1=qs_col[:].unsqueeze(1).to_broadcast([P, P, PACK]), op=ALU.mult)
+
+        def quant_b(c):
+            quantize(b_q, tile_cols(c), b_il[:, tile_cols(c), :].rearrange("p c j -> p (c j)"))
+
+        g_il = {}
+
+        def turn_g(i, pair_):
+            bank = psum.tile([P, 2 * 2 * P], F32, name="gt", bufs=2)
+            for u in range(2):
+                for v in range(2):
+                    t = 2 * pair_ + v
+                    at = (2 * u + v) * P
+                    nc.tensor.transpose(out=bank[:, at:at + P], in_=g_raw[i][:, t, :].bitcast(F32)[:, u:2 * P:2], identity=ident_f[:])
+            return bank
+
+        def load_p(i, pair_, bank):
+            if i not in g_il:
+                g_il[i] = temp([P, ROWS, PACK], BF16, "lay", bufs=7)
+            nc.vector.tensor_tensor(
+                out=g_il[i][:, pair_ * 2 * P:(pair_ + 1) * 2 * P, :].rearrange("p n (u e) -> p n u e", u=2),
+                in0=bank[:].bitcast(BF16).rearrange("p (u n e) -> p n u e", u=2, e=2),
+                in1=p_col[:].rearrange("p (u e) -> p u e", u=2).unsqueeze(1).to_broadcast([P, 2 * P, 2, 2]),
+                op=ALU.mult,
+            )
+
+        def quant_g(i):
+            quantize(g_q[i], every, flat(g_il[i]))
+
+        x_il = {}
+
+        def lay_x(i, h, engine, ts=slice(0, PACK)):
+            if (i, h) not in x_il:
+                x_il[i, h] = temp([P, ROWS, PACK], BF16, "lay", bufs=7)
+            interleave(engine, x_il[i, h], x_raw[i][h], ts)
+
+        def quant_x(i, h):
+            quantize(x_q[i][h], every, flat(x_il[i, h]))
+
+        a_bank, c_bank, ra, rc = {}, {}, {}, {}
+        num, den, y_den, y_num, res = {}, {}, {}, {}, {}
+
+        def mm(i, t):
+            a_bank[i, t] = psum.tile([P, R], F32, name="a_bank", bufs=3)
+            c_bank[i, t] = psum.tile([P, R], F32, name="c_bank", bufs=3)
+            for h in range(HALVES):
+                multiply(a_bank[i, t][:], x_q[i][h], tile_cols(t), fw_q[h], every, h == 0, h == HALVES - 1)
+            multiply(c_bank[i, t][:], g_q[i], tile_cols(t), b_q, every, True, True)
+
+        def natural(bank):
+            return bank[:].rearrange("p (t m) -> p m t", t=PACK)
+
+        def relu(i, t):
+            ra[i, t] = temp([P, R], F32, "ra", bufs=3)
+            rc[i, t] = temp([P, R], F32, "rc", bufs=3)
+            nc.scalar.activation(out=ra[i, t][:].rearrange("p (m t) -> p m t", t=PACK), in_=natural(a_bank[i, t]), func=ACT.Relu, scale=-1.0)
+            nc.scalar.activation(out=rc[i, t][:].rearrange("p (m t) -> p m t", t=PACK), in_=natural(c_bank[i, t]), func=ACT.Relu, scale=-1.0)
+
+        def merge(i, t):
+            if i not in num:
+                num[i] = temp([P, PACK, R], F32, "num", bufs=3)
+                den[i] = temp([P, PACK, R], F32, "den", bufs=3)
+            for dst, bank, part in ((num[i], a_bank[i, t], rc[i, t]), (den[i], c_bank[i, t], ra[i, t])):
+                nc.vector.scalar_tensor_tensor(
+                    out=dst[:, t, :].rearrange("p (m t) -> p m t", t=PACK), in0=natural(bank), scalar=0.0,
+                    in1=part[:].rearrange("p (m t) -> p m t", t=PACK), op0=ALU.max, op1=ALU.add)
+
+        def root(i, ts, which):
+            src, func = (num, ACT.Sqrt) if which == "num" else (den, ACT.Abs_reciprocal_sqrt)
+            nc.scalar.activation(out=src[i][:, ts, :], in_=src[i][:, ts, :], func=func, bias=OFFSET)
+
+        def ratio(i, ts):
+            nc.vector.tensor_tensor(out=num[i][:, ts, :], in0=num[i][:, ts, :], in1=den[i][:, ts, :], op=ALU.mult)
+
+        def update(i, ts):
+            if i not in res:
+                res[i] = temp([P, PACK, R], F32, "res")
+            nc.vector.tensor_tensor(out=res[i][:, ts, :], in0=num[i][:, ts, :], in1=g_raw[i][:, ts, :], op=ALU.mult)
+            nc.sync.dma_start(out=out[i * ROWS:(i + 1) * ROWS, :].rearrange("(m t) r -> m t r", t=PACK)[:, ts, :], in_=res[i][:, ts, :])
+
+        r_il, r_codes = {}, {}
+        r_scales = kept([P, GROUPS, R], U8, "r_scales")
+
+        def lay_r(i, cols, engine):
+            if i not in r_il:
+                r_il[i] = temp([P, R, PACK], BF16, "r_il")
+                r_codes[i] = temp([P, R], U32, "r_codes")
+            o = r_il[i][:, cols, :]
+            s = res[i][:, :, cols].rearrange("p t r -> p r t")
+            if engine == "V":
+                nc.vector.tensor_copy(out=o, in_=s)
+            else:
+                nc.scalar.copy(out=o, in_=s)
+
+        def quant_r(i, cols):
+            nc.vector.quantize_mx(out=r_codes[i][:, cols].bitcast(FP8X4), scales=r_scales[:, i, cols], in_=r_il[i][:, cols, :].rearrange("p c j -> p (c j)"))
+
+        def store_planes(i):
+            nc.sync.dma_start(out=words.rearrange("g k m t -> g k (m t)")[i, :, :].bitcast(I32), in_=r_codes[i][:].bitcast(I32))
+            for Q in range(4):
+                nc.sync.dma_start(out=scales[i, 4 * Q:4 * Q + 4, :].bitcast(I32), in_=r_scales[32 * Q:32 * Q + 4, i, :].bitcast(I32))
+
+        both = [slice(0, 2), slice(2, 4)]
+        lo, hi = both
+        left, right = slice(0, R // 2), slice(R // 2, R)
+        steps = GROUPS * PACK
+        gb = [turn_g(0, 0), turn_g(0, 1)]
+        sign_f(0)
+        interleave("S", f_il[0], fs[0])
+        sign_f(1)
+        nc.vector.scalar_tensor_tensor(out=qs_col[:], in0=s_col[:], scalar=-1.0, in1=q_col[:], op0=ALU.add, op1=ALU.mult)
+        interleave("V", f_il[1], fs[1])
+        lay_x(0, 0, "S")
+        weigh_f(1)
+        quantize(f_q[1], every, flat(f_il[1]))
+        weigh_f(0)
+        quantize(fw_q[1], every, flat(fw_il[1]))
+        quantize(f_q[0], every, flat(f_il[0]))
+        quantize(fw_q[0], every, flat(fw_il[0]))
+        lay_x(0, 1, "S")
+        banks = [gram(c) for c in range(4)]
+        load_p(0, 0, gb[0])
+        load_p(0, 1, gb[1])
+        gain_b(0, banks[0])
+        quant_g(0)
+        gain_b(1, banks[1])
+        quant_b(0)
+        gain_b(2, banks[2])
+        quant_b(1)
+        gain_b(3, banks[3])
+        quant_b(2)
+        quant_x(0, 0)
+        quant_b(3)
+        quant_x(0, 1)
+        lay_x(1, 0, "S")
+
+        def root_piece(i, n):
+            order = ("den", "num") if i % 2 == 0 else ("num", "den")
+            root(i, both[n % 2], order[n // 2])
+
+        mm(0, 0)
+        lay_x(1, 1, "V", hi)
+        for n in range(steps + 1):
+            i, t = divmod(n, PACK)
+            if n + 1 < steps:
+                mm(*divmod(n + 1, PACK))
+            if n < steps:
+                relu(i, t)
+            if n == 0:
+                lay_x(1, 1, "S", lo)
+            if n >= 1:
+                merge(*divmod(n - 1, PACK))
+            if i >= 1 and n < steps:
+                root_piece(i - 1, t)
+            if i + 2 < GROUPS:
+                lay_x(i + 2, t // 2, "VS"[t % 2], both[t % 2])
+            if i + 1 < GROUPS:
+                if t == 0:
+                    gb = [turn_g(i + 1, 0), turn_g(i + 1, 1)]
+                    quant_x(i + 1, 0)
+                if t == 1:
+                    load_p(i + 1, 0, gb[0])
+                    load_p(i + 1, 1, gb[1])
+                    quant_x(i + 1, 1)
+                if t == 2:
+                    quant_g(i + 1)
+            if t == 3 and i >= 1:
+                ratio(i - 1, both[0])
+            if i >= 2:
+                if t == 0:
+                    ratio(i - 2, both[1])
+                    update(i - 2, both[0])
+                if t == 1:
+                    update(i - 2, both[1])
+                if t == 2:
+                    lay_r(i - 2, left, "V")
+                    lay_r(i - 2, right, "S")
+                if t == 3:
+                    quant_r(i - 2, slice(0, R))
+                    store_planes(i - 2)
+        i = GROUPS - 1
+        for n in range(4):
+            root_piece(i, n)
+        update(i - 1, both[1])
+        lay_r(i - 1, slice(0, R), "V")
+        for ts in both:
+            ratio(i, ts)
+        quant_r(i - 1, slice(0, R))
+        store_planes(i - 1)
+        for ts in both:
+            update(i, ts)
+        lay_r(i, slice(0, R // 2), "V")
+        lay_r(i, slice(R // 2, R), "S")
+        quant_r(i, slice(0, R // 2))
+        quant_r(i, slice(R // 2, R))
+        store_planes(i)

@@ -1,3 +1,4 @@
+CFG = {"f0":"S","f1":"S","x00":"S","x01":"S","x10":"S","x11":"V","x20":"V","x21":"S","x30":"V","x31":"V","e11":1,"r0":"V","G":1,"gt":0,"g3":0,"warm":1,"r2":"V","t0":"V","t1":"S","mfirst":0}
 from contextlib import ExitStack
 
 import concourse.mybir as mybir
@@ -60,15 +61,16 @@ def tile_weightedsignedseminmfupdate_x1_kernel(tc, x, f, w, g, p, q, out, words,
         make_identity(nc, ident_b[:])
         make_identity(nc, ident_f[:])
 
+        ctx.enter_context(tc.manual_schedule())
 
         nc.sync.dma_start(out=p_col[:], in_=p.rearrange("(k t) -> k t", t=PACK))
         load_f(0)
         load_f(1)
         nc.sync.dma_start(out=w_col[:], in_=w.rearrange("(h k j) -> k h j", h=HALVES, j=PACK))
         nc.sync.dma_start(out=q_col[:], in_=q.rearrange("(k t) -> k t", t=PACK))
+        load_g(0)
         load_x(0, 0)
         load_x(0, 1)
-        load_g(0)
         for i in range(1, GROUPS):
             load_g(i)
             load_x(i, 0)
@@ -102,12 +104,12 @@ def tile_weightedsignedseminmfupdate_x1_kernel(tc, x, f, w, g, p, q, out, words,
         def tile_cols(t):
             return slice(t * P, (t + 1) * P)
 
-        s_bank = psum.tile([P, R], F32, name="gt", bufs=2)
+        s_bank = psum.tile([P, 2 * R], BF16, name="gt", bufs=2)[:, 0:R]
         for t in range(PACK):
-            nc.tensor.matmul(out=s_bank[:, tile_cols(t)], lhsT=p_col[:, t:t + 1].to_broadcast([P, P]), rhs=ident_b[:], start=True, stop=True)
+            nc.tensor.transpose(out=s_bank[:, tile_cols(t)], in_=p_col[:, t:t + 1].to_broadcast([P, P]), identity=ident_b[:])
         s_two = kept([P, R], BF16, "s_two")
         s_row = kept([P, R], BF16, "s_row")
-        nc.vector.tensor_scalar(out=s_two[:].rearrange("p (m t) -> p m t", t=PACK), in0=s_bank[:].rearrange("p (t m) -> p m t", t=PACK), scalar1=0.0, scalar2=2.0, op0=ALU.is_ge, op1=ALU.mult)
+        nc.vector.tensor_scalar(out=s_two[:].rearrange("p (m t) -> p m t", t=PACK), in0=s_bank.rearrange("p (t m) -> p m t", t=PACK), scalar1=0.0, scalar2=2.0, op0=ALU.is_ge, op1=ALU.mult)
         s_col = kept([P, PACK], F32, "s_col")
         qs_col = kept([P, PACK], F32, "qs_col")
         nc.vector.tensor_scalar(out=s_col[:], in0=p_col[:], scalar1=0.0, scalar2=2.0, op0=ALU.is_ge, op1=ALU.mult)
@@ -178,7 +180,22 @@ def tile_weightedsignedseminmfupdate_x1_kernel(tc, x, f, w, g, p, q, out, words,
         def lay_x(i, h, engine, ts=slice(0, PACK)):
             if (i, h) not in x_il:
                 x_il[i, h] = temp([P, ROWS, PACK], BF16, "lay", bufs=7)
-            interleave(engine, x_il[i, h], x_raw[i][h], ts)
+            if len(engine) == 1:
+                interleave(engine, x_il[i, h], x_raw[i][h], ts)
+                return
+            for c in range(ts.start // 2, ts.stop // 2):
+                bank = psum.tile([P, 2 * P * PACK], BF16, name="gt", bufs=2)
+                for j in range(PACK):
+                    nc.tensor.matmul(
+                        out=bank[:].rearrange("p (t m j) -> p t m j", t=2, j=PACK)[:, :, :, j],
+                        lhsT=ident_b[:],
+                        rhs=x_raw[i][h][:, j, :].rearrange("p (m t) -> p t m", t=PACK)[:, 2 * c:2 * c + 2, :],
+                        start=True, stop=True)
+                dst = x_il[i, h][:, 2 * c * P:2 * (c + 1) * P, :].rearrange("p c j -> p (c j)")
+                if engine == "PV":
+                    nc.vector.tensor_copy(out=dst, in_=bank[:])
+                else:
+                    nc.scalar.copy(out=dst, in_=bank[:])
 
         def quant_x(i, h):
             quantize(x_q[i][h], every, flat(x_il[i, h]))
@@ -211,23 +228,25 @@ def tile_weightedsignedseminmfupdate_x1_kernel(tc, x, f, w, g, p, q, out, words,
                     out=dst[:, t, :].rearrange("p (m t) -> p m t", t=PACK), in0=natural(bank), scalar=0.0,
                     in1=part[:].rearrange("p (m t) -> p m t", t=PACK), op0=ALU.max, op1=ALU.add)
 
-        def root(i, ts, which):
+        def root(i, ts, which, cols=slice(0, R)):
             src, func = (num, ACT.Sqrt) if which == "num" else (den, ACT.Abs_reciprocal_sqrt)
-            nc.scalar.activation(out=src[i][:, ts, :], in_=src[i][:, ts, :], func=func, bias=OFFSET)
+            nc.scalar.activation(out=src[i][:, ts, cols], in_=src[i][:, ts, cols], func=func, bias=OFFSET)
 
-        def ratio(i, ts):
-            nc.vector.tensor_tensor(out=num[i][:, ts, :], in0=num[i][:, ts, :], in1=den[i][:, ts, :], op=ALU.mult)
+        def ratio(i, ts, cols=slice(0, R)):
+            nc.vector.tensor_tensor(out=num[i][:, ts, cols], in0=num[i][:, ts, cols], in1=den[i][:, ts, cols], op=ALU.mult)
 
-        def update(i, ts):
+        def update(i, ts, engine=nc.vector, cols=slice(0, R)):
             if i not in res:
                 res[i] = temp([P, PACK, R], F32, "res")
-            nc.vector.tensor_tensor(out=res[i][:, ts, :], in0=num[i][:, ts, :], in1=g_raw[i][:, ts, :], op=ALU.mult)
-            nc.sync.dma_start(out=out[i * ROWS:(i + 1) * ROWS, :].rearrange("(m t) r -> m t r", t=PACK)[:, ts, :], in_=res[i][:, ts, :])
+            engine.tensor_tensor(out=res[i][:, ts, cols], in0=num[i][:, ts, cols], in1=g_raw[i][:, ts, cols], op=ALU.mult)
+
+        def store_out(i, ts, cols=slice(0, R)):
+            nc.sync.dma_start(out=out[i * ROWS:(i + 1) * ROWS, :].rearrange("(m t) r -> m t r", t=PACK)[:, ts, cols], in_=res[i][:, ts, cols])
 
         r_il, r_codes = {}, {}
         r_scales = kept([P, GROUPS, R], U8, "r_scales")
 
-        def lay_r(i, cols, engine):
+        def lay_r(i, cols, engine="V"):
             if i not in r_il:
                 r_il[i] = temp([P, R, PACK], BF16, "r_il")
                 r_codes[i] = temp([P, R], U32, "r_codes")
@@ -246,97 +265,111 @@ def tile_weightedsignedseminmfupdate_x1_kernel(tc, x, f, w, g, p, q, out, words,
             for Q in range(4):
                 nc.sync.dma_start(out=scales[i, 4 * Q:4 * Q + 4, :].bitcast(I32), in_=r_scales[32 * Q:32 * Q + 4, i, :].bitcast(I32))
 
-        both = [slice(0, 2), slice(2, 4)]
-        lo, hi = both
+        lo, hi, four = slice(0, 2), slice(2, 4), slice(0, 4)
         left, right = slice(0, R // 2), slice(R // 2, R)
-        steps = GROUPS * PACK
+        G_ = nc.gpsimd if CFG.get("G", 1) else nc.vector
+        if CFG.get("warm", 1):
+            warm = kept([P, 1], F32, "warm")
+            nc.gpsimd.memset(warm[:], 1.0)
+            nc.scalar.activation(out=warm[:], in_=warm[:], func=ACT.Abs_reciprocal_sqrt)
         gb = [turn_g(0, 0), turn_g(0, 1)]
         sign_f(0)
-        interleave("S", f_il[0], fs[0])
+        interleave(CFG["f0"], f_il[0], fs[0])
         sign_f(1)
         nc.vector.scalar_tensor_tensor(out=qs_col[:], in0=s_col[:], scalar=-1.0, in1=q_col[:], op0=ALU.add, op1=ALU.mult)
-        interleave("V", f_il[1], fs[1])
-        lay_x(0, 0, "S")
-        weigh_f(1)
-        quantize(f_q[1], every, flat(f_il[1]))
-        weigh_f(0)
-        quantize(fw_q[1], every, flat(fw_il[1]))
-        quantize(f_q[0], every, flat(f_il[0]))
-        quantize(fw_q[0], every, flat(fw_il[0]))
-        lay_x(0, 1, "S")
-        banks = [gram(c) for c in range(4)]
+        interleave(CFG["f1"], f_il[1], fs[1])
         load_p(0, 0, gb[0])
         load_p(0, 1, gb[1])
-        gain_b(0, banks[0])
+        lay_x(0, 0, CFG["x00"])
+        weigh_f(0)
         quant_g(0)
-        gain_b(1, banks[1])
-        quant_b(0)
-        gain_b(2, banks[2])
-        quant_b(1)
-        gain_b(3, banks[3])
-        quant_b(2)
+        quantize(f_q[0], every, flat(f_il[0]))
+        quantize(fw_q[0], every, flat(fw_il[0]))
+        weigh_f(1)
+        quantize(f_q[1], every, flat(f_il[1]))
+        quantize(fw_q[1], every, flat(fw_il[1]))
+        lay_x(0, 1, CFG["x01"])
+        banks = [gram(c) for c in range(4)]
         quant_x(0, 0)
-        quant_b(3)
+        for c in range(4):
+            gain_b(c, banks[c])
         quant_x(0, 1)
-        lay_x(1, 0, "S")
-
-        def root_piece(i, n):
-            order = ("den", "num") if i % 2 == 0 else ("num", "den")
-            root(i, both[n % 2], order[n // 2])
+        quantize(b_q, every, flat(b_il))
+        lay_x(1, 0, CFG["x10"])
 
         mm(0, 0)
-        lay_x(1, 1, "V", hi)
-        for n in range(steps + 1):
-            i, t = divmod(n, PACK)
-            if n + 1 < steps:
-                mm(*divmod(n + 1, PACK))
-            if n < steps:
-                relu(i, t)
-            if n == 0:
-                lay_x(1, 1, "S", lo)
-            if n >= 1:
-                merge(*divmod(n - 1, PACK))
-            if i >= 1 and n < steps:
-                root_piece(i - 1, t)
-            if i + 2 < GROUPS:
-                lay_x(i + 2, t // 2, "VS"[t % 2], both[t % 2])
+        mm(0, 1)
+        if CFG["e11"]:
+            lay_x(1, 1, CFG["x11"])
+        for s in range(2 * GROUPS):
+            i, c = divmod(s, 2)
+            for v in range(2):
+                relu(i, 2 * c + v)
             if i + 1 < GROUPS:
-                if t == 0:
+                if c == 0:
+                    if i == 0 and not CFG["e11"]:
+                        lay_x(1, 1, CFG["x11"])
                     gb = [turn_g(i + 1, 0), turn_g(i + 1, 1)]
                     quant_x(i + 1, 0)
-                if t == 1:
                     load_p(i + 1, 0, gb[0])
                     load_p(i + 1, 1, gb[1])
-                    quant_x(i + 1, 1)
-                if t == 2:
+                else:
                     quant_g(i + 1)
-            if t == 3 and i >= 1:
-                ratio(i - 1, both[0])
+                    quant_x(i + 1, 1)
+            if i >= 3 and c == 0:
+                lay_r(i - 3, every, CFG["r0"])
+            if i >= 3 and c == 1:
+                quant_r(i - 3, every)
+                store_planes(i - 3)
+            if i >= 1:
+                order = ("den", "num") if i % 2 else ("num", "den")
+                root(i - 1, four, order[c])
+            if i + 2 < GROUPS:
+                lay_x(i + 2, c, CFG["x%d%d" % (i + 2, c)])
+            if CFG.get("mfirst"):
+                for v in range(2):
+                    merge(i, 2 * c + v)
             if i >= 2:
-                if t == 0:
-                    ratio(i - 2, both[1])
-                    update(i - 2, both[0])
-                if t == 1:
-                    update(i - 2, both[1])
-                if t == 2:
-                    lay_r(i - 2, left, "V")
-                    lay_r(i - 2, right, "S")
-                if t == 3:
-                    quant_r(i - 2, slice(0, R))
-                    store_planes(i - 2)
+                half = (lo, hi)[c]
+                ratio(i - 2, half)
+                update(i - 2, half, G_)
+                store_out(i - 2, half)
+            if not CFG.get("mfirst"):
+                for v in range(2):
+                    merge(i, 2 * c + v)
+            nxt = 2 * s + 2
+            for v in range(2):
+                if nxt + v < GROUPS * PACK:
+                    mm(*divmod(nxt + v, PACK))
         i = GROUPS - 1
-        for n in range(4):
-            root_piece(i, n)
-        update(i - 1, both[1])
-        lay_r(i - 1, slice(0, R), "V")
-        for ts in both:
-            ratio(i, ts)
-        quant_r(i - 1, slice(0, R))
+        parts = [left, slice(256, 384), slice(384, 512)]
+        root(i, four, "num")
+        ratio(i - 1, lo)
+        update(i - 1, lo, G_)
+        lay_r(i - 2, every)
+        store_out(i - 1, lo)
+        ratio(i - 1, hi)
+        quant_r(i - 2, every)
+        store_planes(i - 2)
+        update(i - 1, hi, nc.gpsimd if CFG.get("gt") else nc.vector)
+        store_out(i - 1, hi)
+        for cols in parts:
+            root(i, four, "den", cols)
+        lay_r(i - 1, every, CFG.get("r2", "V"))
+        ratio(i, four, parts[0])
+        quant_r(i - 1, every)
         store_planes(i - 1)
-        for ts in both:
-            update(i, ts)
-        lay_r(i, slice(0, R // 2), "V")
-        lay_r(i, slice(R // 2, R), "S")
-        quant_r(i, slice(0, R // 2))
-        quant_r(i, slice(R // 2, R))
+        update(i, four, nc.gpsimd if CFG.get("g3") else nc.vector, parts[0])
+        store_out(i, four, parts[0])
+        ratio(i, four, parts[1])
+        update(i, four, nc.vector, parts[1])
+        lay_r(i, parts[0], CFG.get("t0", "V"))
+        ratio(i, four, parts[2])
+        lay_r(i, parts[1], CFG.get("t1", "V"))
+        update(i, four, nc.vector, parts[2])
+        store_out(i, four, right)
+        quant_r(i, parts[0])
+        lay_r(i, parts[2])
+        quant_r(i, parts[1])
+        quant_r(i, parts[2])
         store_planes(i)

@@ -1,4 +1,4 @@
-CFG = {"f0":"S","f1":"S","x00":"S","x01":"S","x10":"S","x11":"V","x20":"V","x21":"S","x30":"V","x31":"V","e11":1,"r0":"V","G":1,"gt":0,"g3":0,"warm":1,"r2":"V","t0":"V","t1":"S","mfirst":0}
+CFG = {"f0":"S","f1":"S","x00":"S","x01":"S","x10":"S","x11":"V","x20":"V","x21":"S","x30":"V","x31":"V","e11":0,"r0":"V","r1":"V","r2":"S","t0":"S","t1":"S","G":1,"gt":0,"g3":0,"warm":1,"mfirst":0}
 from contextlib import ExitStack
 
 import concourse.mybir as mybir
@@ -104,7 +104,7 @@ def tile_weightedsignedseminmfupdate_x1_kernel(tc, x, f, w, g, p, q, out, words,
         def tile_cols(t):
             return slice(t * P, (t + 1) * P)
 
-        s_bank = psum.tile([P, 2 * R], BF16, name="gt", bufs=2)[:, 0:R]
+        s_bank = psum.tile([P, 2 * R], BF16, name="bank", bufs=8)[:, 0:R]
         for t in range(PACK):
             nc.tensor.transpose(out=s_bank[:, tile_cols(t)], in_=p_col[:, t:t + 1].to_broadcast([P, P]), identity=ident_b[:])
         s_two = kept([P, R], BF16, "s_two")
@@ -122,13 +122,15 @@ def tile_weightedsignedseminmfupdate_x1_kernel(tc, x, f, w, g, p, q, out, words,
         def sign_f(h):
             nc.vector.tensor_tensor(out=fs[h][:], in0=f_raw[h][:], in1=s_row[:].unsqueeze(1).to_broadcast([P, PACK, R]), op=ALU.mult)
 
-        def interleave(engine, dst, src, ts=slice(0, PACK)):
-            o = dst[:].rearrange("p (t m) j -> p t m j", t=PACK)[:, ts, :, :]
-            i = src[:].rearrange("p j (m t) -> p t m j", t=PACK)[:, ts, :, :]
+        def interleave(engine, dst, src):
             if engine == "V":
-                nc.vector.tensor_copy(out=o, in_=i)
+                nc.vector.tensor_copy(
+                    out=dst[:].rearrange("p (t b c) j -> p b t (c j)", t=PACK, c=2).rearrange("p b t (c j) -> p b t c j", c=2) if not CFG.get("v3") else dst[:].rearrange("p (t m) j -> p m t j", t=PACK),
+                    in_=src[:].rearrange("p j (b c t) -> p b t c j", t=PACK, c=2) if not CFG.get("v3") else src[:].rearrange("p j (m t) -> p m t j", t=PACK))
             else:
-                nc.scalar.copy(out=o, in_=i)
+                nc.scalar.copy(
+                    out=dst[:].rearrange("p (t m) j -> p m t j", t=PACK),
+                    in_=src[:].rearrange("p j (m t) -> p m t j", t=PACK))
 
         def weigh_f(h):
             nc.vector.tensor_tensor(out=fw_il[h][:], in0=f_il[h][:], in1=w_col[:, h, :].unsqueeze(1).to_broadcast([P, R, PACK]), op=ALU.mult)
@@ -137,7 +139,7 @@ def tile_weightedsignedseminmfupdate_x1_kernel(tc, x, f, w, g, p, q, out, words,
             return t[:].rearrange("p c j -> p (c j)")
 
         def gram(c):
-            bank = psum.tile([P, PACK, P], F32, name=("a_bank", "c_bank")[c % 2], bufs=3)
+            bank = psum.tile([P, PACK, P], F32, name="bank", bufs=8)
             for t in range(PACK):
                 for h in range(HALVES):
                     multiply(bank[:, t, :], f_q[h], tile_cols(t), fw_q[h], tile_cols(c), h == 0, h == HALVES - 1)
@@ -154,7 +156,7 @@ def tile_weightedsignedseminmfupdate_x1_kernel(tc, x, f, w, g, p, q, out, words,
         g_il = {}
 
         def turn_g(i, pair_):
-            bank = psum.tile([P, 2 * 2 * P], F32, name="gt", bufs=2)
+            bank = psum.tile([P, 2 * 2 * P], F32, name="bank", bufs=8)
             for u in range(2):
                 for v in range(2):
                     t = 2 * pair_ + v
@@ -181,10 +183,10 @@ def tile_weightedsignedseminmfupdate_x1_kernel(tc, x, f, w, g, p, q, out, words,
             if (i, h) not in x_il:
                 x_il[i, h] = temp([P, ROWS, PACK], BF16, "lay", bufs=7)
             if len(engine) == 1:
-                interleave(engine, x_il[i, h], x_raw[i][h], ts)
+                interleave(engine, x_il[i, h], x_raw[i][h])
                 return
             for c in range(ts.start // 2, ts.stop // 2):
-                bank = psum.tile([P, 2 * P * PACK], BF16, name="gt", bufs=2)
+                bank = psum.tile([P, 2 * P * PACK], BF16, name="bank", bufs=8)
                 for j in range(PACK):
                     nc.tensor.matmul(
                         out=bank[:].rearrange("p (t m j) -> p t m j", t=2, j=PACK)[:, :, :, j],
@@ -204,8 +206,8 @@ def tile_weightedsignedseminmfupdate_x1_kernel(tc, x, f, w, g, p, q, out, words,
         num, den, y_den, y_num, res = {}, {}, {}, {}, {}
 
         def mm(i, t):
-            a_bank[i, t] = psum.tile([P, R], F32, name="a_bank", bufs=3)
-            c_bank[i, t] = psum.tile([P, R], F32, name="c_bank", bufs=3)
+            a_bank[i, t] = psum.tile([P, R], F32, name="bank", bufs=8)
+            c_bank[i, t] = psum.tile([P, R], F32, name="bank", bufs=8)
             for h in range(HALVES):
                 multiply(a_bank[i, t][:], x_q[i][h], tile_cols(t), fw_q[h], every, h == 0, h == HALVES - 1)
             multiply(c_bank[i, t][:], g_q[i], tile_cols(t), b_q, every, True, True)
@@ -342,34 +344,47 @@ def tile_weightedsignedseminmfupdate_x1_kernel(tc, x, f, w, g, p, q, out, words,
                 if nxt + v < GROUPS * PACK:
                     mm(*divmod(nxt + v, PACK))
         i = GROUPS - 1
-        parts = [left, slice(256, 384), slice(384, 512)]
+        parts = [slice(0, 256), slice(256, 384), slice(384, 512)]
         root(i, four, "num")
         ratio(i - 1, lo)
         update(i - 1, lo, G_)
-        lay_r(i - 2, every)
         store_out(i - 1, lo)
+        if CFG["r1"] == "V":
+            lay_r(i - 2, every, "V")
         ratio(i - 1, hi)
-        quant_r(i - 2, every)
-        store_planes(i - 2)
-        update(i - 1, hi, nc.gpsimd if CFG.get("gt") else nc.vector)
+        update(i - 1, hi, nc.gpsimd if CFG["gt"] else nc.vector)
         store_out(i - 1, hi)
         for cols in parts:
             root(i, four, "den", cols)
-        lay_r(i - 1, every, CFG.get("r2", "V"))
+        if CFG["r1"] == "S":
+            lay_r(i - 2, every, "S")
+        if CFG["r2"] == "V":
+            lay_r(i - 1, every, "V")
         ratio(i, four, parts[0])
-        quant_r(i - 1, every)
-        store_planes(i - 1)
-        update(i, four, nc.gpsimd if CFG.get("g3") else nc.vector, parts[0])
+        quant_r(i - 2, every)
+        store_planes(i - 2)
+        if CFG["r2"] == "S":
+            lay_r(i - 1, every, "S")
+        update(i, four, nc.gpsimd if CFG["g3"] else nc.vector, parts[0])
         store_out(i, four, parts[0])
         ratio(i, four, parts[1])
+        if CFG["r2"] == "V":
+            quant_r(i - 1, every)
+            store_planes(i - 1)
         update(i, four, nc.vector, parts[1])
-        lay_r(i, parts[0], CFG.get("t0", "V"))
+        if CFG["t0"] == "V":
+            lay_r(i, parts[0], "V")
         ratio(i, four, parts[2])
-        lay_r(i, parts[1], CFG.get("t1", "V"))
+        if CFG["t0"] == "S":
+            lay_r(i, parts[0], "S")
+        if CFG["r2"] == "S":
+            quant_r(i - 1, every)
+            store_planes(i - 1)
+        lay_r(i, parts[1], CFG["t1"])
         update(i, four, nc.vector, parts[2])
         store_out(i, four, right)
         quant_r(i, parts[0])
-        lay_r(i, parts[2])
+        lay_r(i, parts[2], "V")
         quant_r(i, parts[1])
         quant_r(i, parts[2])
         store_planes(i)

@@ -1,4 +1,5 @@
-CFG = {"f0":"S","f1":"S","x00":"S","x01":"S","x10":"S","x11":"V","x20":"V","x21":"S","x30":"V","x31":"V","e11":0,"r0":"V","r1":"V","r2":"S","t0":"S","t1":"S","G":1,"gt":0,"g3":0,"warm":1,"mfirst":0}
+CFG = {"f0":"S","f1":"S","x00":"S","x01":"S","x10":"G","x11":"S","x20":"G","x21":"G","x30":"G","x31":"G","e11":0,"r0":"V","r1":"V","r2":"S","t0":"S","t1":"S","gt":0,"g3":0,"sc":"S","qx":2,"lp0":1,"lp1":0,"lp2":0,"vr0":0,"vr1":0,"vr2":0,"vr3":1,"vr4":0,"vr5":1,"vr6":0,"vr7":1}
+NLAY = 6
 from contextlib import ExitStack
 
 import concourse.mybir as mybir
@@ -104,20 +105,28 @@ def tile_weightedsignedseminmfupdate_x1_kernel(tc, x, f, w, g, p, q, out, words,
         def tile_cols(t):
             return slice(t * P, (t + 1) * P)
 
-        s_bank = psum.tile([P, 2 * R], BF16, name="bank", bufs=8)[:, 0:R]
-        for t in range(PACK):
-            nc.tensor.transpose(out=s_bank[:, tile_cols(t)], in_=p_col[:, t:t + 1].to_broadcast([P, P]), identity=ident_b[:])
-        s_two = kept([P, R], BF16, "s_two")
-        s_row = kept([P, R], BF16, "s_row")
-        nc.vector.tensor_scalar(out=s_two[:].rearrange("p (m t) -> p m t", t=PACK), in0=s_bank.rearrange("p (t m) -> p m t", t=PACK), scalar1=0.0, scalar2=2.0, op0=ALU.is_ge, op1=ALU.mult)
-        s_col = kept([P, PACK], F32, "s_col")
+        warm = kept([P, 1], F32, "warm")
+        nc.gpsimd.memset(warm[:], 1.0)
+        nc.scalar.activation(out=warm[:], in_=warm[:], func=ACT.Abs_reciprocal_sqrt)
+
+        s_two = kept([P, PACK], F32, "s_two")
+        s_col = kept([P, PACK], BF16, "s_col")
         qs_col = kept([P, PACK], F32, "qs_col")
-        nc.vector.tensor_scalar(out=s_col[:], in0=p_col[:], scalar1=0.0, scalar2=2.0, op0=ALU.is_ge, op1=ALU.mult)
-        nc.vector.tensor_scalar(out=s_row[:], in0=s_two[:], scalar1=1.0, scalar2=None, op0=ALU.subtract)
+        s_row = kept([P, R], BF16, "s_row")
+        nc.vector.tensor_scalar(out=s_two[:], in0=p_col[:], scalar1=0.0, scalar2=2.0, op0=ALU.is_ge, op1=ALU.mult)
+        nc.vector.tensor_scalar(out=s_col[:], in0=s_two[:], scalar1=1.0, scalar2=None, op0=ALU.subtract)
+        s_bank = psum.tile([P, 2 * R], BF16, name="bank", bufs=8)
+        for t in range(PACK):
+            nc.tensor.transpose(out=s_bank[:, tile_cols(t)], in_=s_col[:, t:t + 1].to_broadcast([P, P]), identity=ident_b[:])
+        s_out, s_in = s_row[:].rearrange("p (m t) -> p m t", t=PACK), s_bank[:, 0:R].rearrange("p (t m) -> p m t", t=PACK)
+        if CFG["sc"] == "S":
+            nc.scalar.copy(out=s_out, in_=s_in)
+        else:
+            nc.vector.tensor_copy(out=s_out, in_=s_in)
 
         fs = f_raw
-        f_il = [temp([P, R, PACK], BF16, "lay", bufs=7) for h in range(HALVES)]
-        fw_il = [temp([P, R, PACK], BF16, "lay", bufs=7) for h in range(HALVES)]
+        f_il = [temp([P, R, PACK], BF16, "lay", bufs=NLAY) for h in range(HALVES)]
+        fw_il = [temp([P, R, PACK], BF16, "lay", bufs=NLAY) for h in range(HALVES)]
 
         def sign_f(h):
             nc.vector.tensor_tensor(out=fs[h][:], in0=f_raw[h][:], in1=s_row[:].unsqueeze(1).to_broadcast([P, PACK, R]), op=ALU.mult)
@@ -145,7 +154,7 @@ def tile_weightedsignedseminmfupdate_x1_kernel(tc, x, f, w, g, p, q, out, words,
                     multiply(bank[:, t, :], f_q[h], tile_cols(t), fw_q[h], tile_cols(c), h == 0, h == HALVES - 1)
             return bank
 
-        b_il = temp([P, R, PACK], BF16, "lay", bufs=7)
+        b_il = temp([P, R, PACK], BF16, "lay", bufs=NLAY)
 
         def gain_b(c, bank):
             nc.vector.tensor_tensor(out=b_il[:, tile_cols(c), :], in0=bank[:].rearrange("p t r -> p r t"), in1=qs_col[:].unsqueeze(1).to_broadcast([P, P, PACK]), op=ALU.mult)
@@ -166,7 +175,7 @@ def tile_weightedsignedseminmfupdate_x1_kernel(tc, x, f, w, g, p, q, out, words,
 
         def load_p(i, pair_, bank):
             if i not in g_il:
-                g_il[i] = temp([P, ROWS, PACK], BF16, "lay", bufs=7)
+                g_il[i] = temp([P, ROWS, PACK], BF16, "lay", bufs=NLAY)
             nc.vector.tensor_tensor(
                 out=g_il[i][:, pair_ * 2 * P:(pair_ + 1) * 2 * P, :].rearrange("p n (u e) -> p n u e", u=2),
                 in0=bank[:].bitcast(BF16).rearrange("p (u n e) -> p n u e", u=2, e=2),
@@ -179,25 +188,16 @@ def tile_weightedsignedseminmfupdate_x1_kernel(tc, x, f, w, g, p, q, out, words,
 
         x_il = {}
 
-        def lay_x(i, h, engine, ts=slice(0, PACK)):
-            if (i, h) not in x_il:
-                x_il[i, h] = temp([P, ROWS, PACK], BF16, "lay", bufs=7)
-            if len(engine) == 1:
-                interleave(engine, x_il[i, h], x_raw[i][h])
+        def lay_x(i, h, engine):
+            slot = "lay" if (i, h) == (0, 1) else ("x_even", "x_odd")[h]
+            x_il[i, h] = temp([P, ROWS, PACK], BF16, slot, bufs=NLAY if slot == "lay" else 1)
+            if engine == "G":
+                nc.gpsimd.tensor_scalar(
+                    out=x_il[i, h][:].rearrange("p (t m) j -> p m t j", t=PACK),
+                    in0=x_raw[i][h][:].rearrange("p j (m t) -> p m t j", t=PACK),
+                    scalar1=1.0, scalar2=0.0, op0=ALU.mult, op1=ALU.add)
                 return
-            for c in range(ts.start // 2, ts.stop // 2):
-                bank = psum.tile([P, 2 * P * PACK], BF16, name="bank", bufs=8)
-                for j in range(PACK):
-                    nc.tensor.matmul(
-                        out=bank[:].rearrange("p (t m j) -> p t m j", t=2, j=PACK)[:, :, :, j],
-                        lhsT=ident_b[:],
-                        rhs=x_raw[i][h][:, j, :].rearrange("p (m t) -> p t m", t=PACK)[:, 2 * c:2 * c + 2, :],
-                        start=True, stop=True)
-                dst = x_il[i, h][:, 2 * c * P:2 * (c + 1) * P, :].rearrange("p c j -> p (c j)")
-                if engine == "PV":
-                    nc.vector.tensor_copy(out=dst, in_=bank[:])
-                else:
-                    nc.scalar.copy(out=dst, in_=bank[:])
+            interleave(engine, x_il[i, h], x_raw[i][h])
 
         def quant_x(i, h):
             quantize(x_q[i][h], every, flat(x_il[i, h]))
@@ -205,30 +205,40 @@ def tile_weightedsignedseminmfupdate_x1_kernel(tc, x, f, w, g, p, q, out, words,
         a_bank, c_bank, ra, rc = {}, {}, {}, {}
         num, den, y_den, y_num, res = {}, {}, {}, {}, {}
 
-        def mm(i, t):
-            a_bank[i, t] = psum.tile([P, R], F32, name="bank", bufs=8)
-            c_bank[i, t] = psum.tile([P, R], F32, name="bank", bufs=8)
-            for h in range(HALVES):
-                multiply(a_bank[i, t][:], x_q[i][h], tile_cols(t), fw_q[h], every, h == 0, h == HALVES - 1)
-            multiply(c_bank[i, t][:], g_q[i], tile_cols(t), b_q, every, True, True)
+        def mm(i, ts):
+            for t in ts:
+                a_bank[i, t] = psum.tile([P, R], F32, name="bank", bufs=8)
+                for h in range(HALVES):
+                    multiply(a_bank[i, t][:], x_q[i][h], tile_cols(t), fw_q[h], every, h == 0, h == HALVES - 1)
+            for t in ts:
+                c_bank[i, t] = psum.tile([P, R], F32, name="bank", bufs=8)
+                multiply(c_bank[i, t][:], g_q[i], tile_cols(t), b_q, every, True, True)
 
         def natural(bank):
             return bank[:].rearrange("p (t m) -> p m t", t=PACK)
 
-        def relu(i, t):
-            ra[i, t] = temp([P, R], F32, "ra", bufs=3)
-            rc[i, t] = temp([P, R], F32, "rc", bufs=3)
-            nc.scalar.activation(out=ra[i, t][:].rearrange("p (m t) -> p m t", t=PACK), in_=natural(a_bank[i, t]), func=ACT.Relu, scale=-1.0)
-            nc.scalar.activation(out=rc[i, t][:].rearrange("p (m t) -> p m t", t=PACK), in_=natural(c_bank[i, t]), func=ACT.Relu, scale=-1.0)
+        def by_four(tile_):
+            return tile_[:].rearrange("p (m t) -> p m t", t=PACK)
 
-        def merge(i, t):
+        def relu(i, ts, on_vector=()):
+            for part, bank, nm in ((ra, a_bank, "ra"), (rc, c_bank, "rc")):
+                for t in ts:
+                    part[i, t] = temp([P, R], F32, nm, bufs=4)
+                    if (nm, t % 2) not in on_vector:
+                        nc.scalar.activation(out=by_four(part[i, t]), in_=natural(bank[i, t]), func=ACT.Relu, scale=-1.0)
+
+        def relu_v(i, t, nm):
+            part, bank = (ra, a_bank) if nm == "ra" else (rc, c_bank)
+            nc.vector.tensor_scalar(out=by_four(part[i, t]), in0=natural(bank[i, t]), scalar1=0.0, scalar2=-1.0, op0=ALU.min, op1=ALU.mult)
+
+        def merge(i, t, first="num"):
             if i not in num:
                 num[i] = temp([P, PACK, R], F32, "num", bufs=3)
                 den[i] = temp([P, PACK, R], F32, "den", bufs=3)
             for dst, bank, part in ((num[i], a_bank[i, t], rc[i, t]), (den[i], c_bank[i, t], ra[i, t])):
                 nc.vector.scalar_tensor_tensor(
                     out=dst[:, t, :].rearrange("p (m t) -> p m t", t=PACK), in0=natural(bank), scalar=0.0,
-                    in1=part[:].rearrange("p (m t) -> p m t", t=PACK), op0=ALU.max, op1=ALU.add)
+                    in1=by_four(part), op0=ALU.max, op1=ALU.add)
 
         def root(i, ts, which, cols=slice(0, R)):
             src, func = (num, ACT.Sqrt) if which == "num" else (den, ACT.Abs_reciprocal_sqrt)
@@ -262,23 +272,24 @@ def tile_weightedsignedseminmfupdate_x1_kernel(tc, x, f, w, g, p, q, out, words,
         def quant_r(i, cols):
             nc.vector.quantize_mx(out=r_codes[i][:, cols].bitcast(FP8X4), scales=r_scales[:, i, cols], in_=r_il[i][:, cols, :].rearrange("p c j -> p (c j)"))
 
-        def store_planes(i):
-            nc.sync.dma_start(out=words.rearrange("g k m t -> g k (m t)")[i, :, :].bitcast(I32), in_=r_codes[i][:].bitcast(I32))
+        def store_words(i, cols):
+            nc.sync.dma_start(out=words.rearrange("g k m t -> g k (m t)")[i, :, :].bitcast(I32)[:, cols], in_=r_codes[i][:, cols].bitcast(I32))
+
+        def store_scales(i):
             for Q in range(4):
                 nc.sync.dma_start(out=scales[i, 4 * Q:4 * Q + 4, :].bitcast(I32), in_=r_scales[32 * Q:32 * Q + 4, i, :].bitcast(I32))
 
+        def store_planes(i):
+            store_words(i, every)
+            store_scales(i)
+
         lo, hi, four = slice(0, 2), slice(2, 4), slice(0, 4)
-        left, right = slice(0, R // 2), slice(R // 2, R)
-        G_ = nc.gpsimd if CFG.get("G", 1) else nc.vector
-        if CFG.get("warm", 1):
-            warm = kept([P, 1], F32, "warm")
-            nc.gpsimd.memset(warm[:], 1.0)
-            nc.scalar.activation(out=warm[:], in_=warm[:], func=ACT.Abs_reciprocal_sqrt)
+        right = slice(R // 2, R)
         gb = [turn_g(0, 0), turn_g(0, 1)]
         sign_f(0)
         interleave(CFG["f0"], f_il[0], fs[0])
         sign_f(1)
-        nc.vector.scalar_tensor_tensor(out=qs_col[:], in0=s_col[:], scalar=-1.0, in1=q_col[:], op0=ALU.add, op1=ALU.mult)
+        nc.vector.tensor_tensor(out=qs_col[:], in0=s_col[:], in1=q_col[:], op=ALU.mult)
         interleave(CFG["f1"], f_il[1], fs[1])
         load_p(0, 0, gb[0])
         load_p(0, 1, gb[1])
@@ -293,61 +304,65 @@ def tile_weightedsignedseminmfupdate_x1_kernel(tc, x, f, w, g, p, q, out, words,
         lay_x(0, 1, CFG["x01"])
         banks = [gram(c) for c in range(4)]
         quant_x(0, 0)
+        if CFG["x11"] == "G":
+            lay_x(1, 1, "G")
         for c in range(4):
             gain_b(c, banks[c])
-        quant_x(0, 1)
+            if c == CFG["qx"]:
+                quant_x(0, 1)
         quantize(b_q, every, flat(b_il))
         lay_x(1, 0, CFG["x10"])
 
-        mm(0, 0)
-        mm(0, 1)
-        if CFG["e11"]:
+        mm(0, (0, 1))
+        VR = [CFG["vr%d" % s] for s in range(8)]
+        if CFG["x11"] != "G" and CFG["e11"]:
             lay_x(1, 1, CFG["x11"])
         for s in range(2 * GROUPS):
             i, c = divmod(s, 2)
-            for v in range(2):
-                relu(i, 2 * c + v)
-            if i + 1 < GROUPS:
-                if c == 0:
-                    if i == 0 and not CFG["e11"]:
-                        lay_x(1, 1, CFG["x11"])
-                    gb = [turn_g(i + 1, 0), turn_g(i + 1, 1)]
-                    quant_x(i + 1, 0)
-                    load_p(i + 1, 0, gb[0])
-                    load_p(i + 1, 1, gb[1])
-                else:
-                    quant_g(i + 1)
-                    quant_x(i + 1, 1)
+            pair_ = (2 * c, 2 * c + 1)
+            onv = [(nm, 1) for nm in ("ra", "rc")[:VR[s]]]
+            relu(i, pair_, onv)
             if i >= 3 and c == 0:
                 lay_r(i - 3, every, CFG["r0"])
             if i >= 3 and c == 1:
                 quant_r(i - 3, every)
                 store_planes(i - 3)
+            if i + 1 < GROUPS:
+                if c == 0:
+                    if i == 0 and CFG["x11"] != "G" and not CFG["e11"]:
+                        lay_x(1, 1, CFG["x11"])
+                    gb = [turn_g(i + 1, 0), turn_g(i + 1, 1)]
+                    if not CFG["lp%d" % i]:
+                        load_p(i + 1, 0, gb[0])
+                        load_p(i + 1, 1, gb[1])
+                else:
+                    quant_g(i + 1)
+                quant_x(i + 1, c)
             if i >= 1:
                 order = ("den", "num") if i % 2 else ("num", "den")
                 root(i - 1, four, order[c])
             if i + 2 < GROUPS:
                 lay_x(i + 2, c, CFG["x%d%d" % (i + 2, c)])
-            if CFG.get("mfirst"):
-                for v in range(2):
-                    merge(i, 2 * c + v)
             if i >= 2:
                 half = (lo, hi)[c]
                 ratio(i - 2, half)
-                update(i - 2, half, G_)
+                update(i - 2, half, nc.gpsimd)
                 store_out(i - 2, half)
-            if not CFG.get("mfirst"):
-                for v in range(2):
-                    merge(i, 2 * c + v)
+            merge(i, 2 * c)
+            for nm, v in onv:
+                relu_v(i, 2 * c + v, nm)
+            merge(i, 2 * c + 1)
+            if i + 1 < GROUPS and c == 0 and CFG["lp%d" % i]:
+                load_p(i + 1, 0, gb[0])
+                load_p(i + 1, 1, gb[1])
             nxt = 2 * s + 2
-            for v in range(2):
-                if nxt + v < GROUPS * PACK:
-                    mm(*divmod(nxt + v, PACK))
+            if nxt < GROUPS * PACK:
+                mm(nxt // PACK, (nxt % PACK, nxt % PACK + 1))
         i = GROUPS - 1
         parts = [slice(0, 256), slice(256, 384), slice(384, 512)]
         root(i, four, "num")
         ratio(i - 1, lo)
-        update(i - 1, lo, G_)
+        update(i - 1, lo, nc.gpsimd)
         store_out(i - 1, lo)
         if CFG["r1"] == "V":
             lay_r(i - 2, every, "V")
@@ -384,7 +399,9 @@ def tile_weightedsignedseminmfupdate_x1_kernel(tc, x, f, w, g, p, q, out, words,
         update(i, four, nc.vector, parts[2])
         store_out(i, four, right)
         quant_r(i, parts[0])
+        store_words(i, parts[0])
         lay_r(i, parts[2], "V")
         quant_r(i, parts[1])
         quant_r(i, parts[2])
-        store_planes(i)
+        store_words(i, right)
+        store_scales(i)

@@ -1,4 +1,4 @@
-CFG = {"f0":"S","f1":"S","x00":"S","x01":"S","x10":"G","x11":"S","x20":"G","x21":"G","x30":"G","x31":"G","e11":0,"r0":"V","r1":"V","r2":"S","t0":"S","t1":"S","gt":0,"g3":0,"sc":"S","qx":2,"lp0":1,"lp1":0,"lp2":0,"vr0":0,"vr1":0,"vr2":0,"vr3":1,"vr4":0,"vr5":1,"vr6":0,"vr7":1}
+CFG = {"f0":"S","f1":"S","x00":"S","x01":"S","x10":"S","x11":"G","x20":"S","x21":"G","x30":"S","x31":"G","e11":1,"r0":"V","r1":"V","r2":"S","t0":"S","t1":"S","gt":0,"g3":0,"sc":"S","qx":2,"lp0":1,"lp1":0,"lp2":0,"vr0":0,"vr1":0,"vr2":0,"vr3":1,"vr4":1,"vr5":1,"vr6":1,"vr7":1,"g2":0,"early":1}
 NLAY = 6
 from contextlib import ExitStack
 
@@ -65,13 +65,16 @@ def tile_weightedsignedseminmfupdate_x1_kernel(tc, x, f, w, g, p, q, out, words,
         ctx.enter_context(tc.manual_schedule())
 
         nc.sync.dma_start(out=p_col[:], in_=p.rearrange("(k t) -> k t", t=PACK))
+        if CFG["x00"] == "V0":
+            load_x(0, 0)
         load_f(0)
         load_f(1)
-        nc.sync.dma_start(out=w_col[:], in_=w.rearrange("(h k j) -> k h j", h=HALVES, j=PACK))
-        nc.sync.dma_start(out=q_col[:], in_=q.rearrange("(k t) -> k t", t=PACK))
         load_g(0)
-        load_x(0, 0)
+        nc.sync.dma_start(out=w_col[:], in_=w.rearrange("(h k j) -> k h j", h=HALVES, j=PACK))
+        if CFG["x00"] != "V0":
+            load_x(0, 0)
         load_x(0, 1)
+        nc.sync.dma_start(out=q_col[:], in_=q.rearrange("(k t) -> k t", t=PACK))
         for i in range(1, GROUPS):
             load_g(i)
             load_x(i, 0)
@@ -262,8 +265,8 @@ def tile_weightedsignedseminmfupdate_x1_kernel(tc, x, f, w, g, p, q, out, words,
             if i not in r_il:
                 r_il[i] = temp([P, R, PACK], BF16, "r_il")
                 r_codes[i] = temp([P, R], U32, "r_codes")
-            o = r_il[i][:, cols, :]
-            s = res[i][:, :, cols].rearrange("p t r -> p r t")
+            o = r_il[i][:, cols, :].rearrange("p (c i) t -> p c t i", i=PACK)
+            s = res[i][:, :, cols].rearrange("p t (c i) -> p c t i", i=PACK)
             if engine == "V":
                 nc.vector.tensor_copy(out=o, in_=s)
             else:
@@ -286,14 +289,16 @@ def tile_weightedsignedseminmfupdate_x1_kernel(tc, x, f, w, g, p, q, out, words,
         lo, hi, four = slice(0, 2), slice(2, 4), slice(0, 4)
         right = slice(R // 2, R)
         gb = [turn_g(0, 0), turn_g(0, 1)]
+        if CFG["x00"] == "V0":
+            lay_x(0, 0, "V")
         sign_f(0)
         interleave(CFG["f0"], f_il[0], fs[0])
         sign_f(1)
-        nc.vector.tensor_tensor(out=qs_col[:], in0=s_col[:], in1=q_col[:], op=ALU.mult)
         interleave(CFG["f1"], f_il[1], fs[1])
         load_p(0, 0, gb[0])
         load_p(0, 1, gb[1])
-        lay_x(0, 0, CFG["x00"])
+        if CFG["x00"] != "V0":
+            lay_x(0, 0, CFG["x00"])
         weigh_f(0)
         quant_g(0)
         quantize(f_q[0], every, flat(f_il[0]))
@@ -302,10 +307,16 @@ def tile_weightedsignedseminmfupdate_x1_kernel(tc, x, f, w, g, p, q, out, words,
         quantize(f_q[1], every, flat(f_il[1]))
         quantize(fw_q[1], every, flat(fw_il[1]))
         lay_x(0, 1, CFG["x01"])
+        if CFG["early"]:
+            gb = [turn_g(1, 0), turn_g(1, 1)]
         banks = [gram(c) for c in range(4)]
         quant_x(0, 0)
+        nc.vector.tensor_tensor(out=qs_col[:], in0=s_col[:], in1=q_col[:], op=ALU.mult)
         if CFG["x11"] == "G":
             lay_x(1, 1, "G")
+        if CFG["early"]:
+            load_p(1, 0, gb[0])
+            load_p(1, 1, gb[1])
         for c in range(4):
             gain_b(c, banks[c])
             if c == CFG["qx"]:
@@ -331,8 +342,9 @@ def tile_weightedsignedseminmfupdate_x1_kernel(tc, x, f, w, g, p, q, out, words,
                 if c == 0:
                     if i == 0 and CFG["x11"] != "G" and not CFG["e11"]:
                         lay_x(1, 1, CFG["x11"])
-                    gb = [turn_g(i + 1, 0), turn_g(i + 1, 1)]
-                    if not CFG["lp%d" % i]:
+                    if i or not CFG["early"]:
+                        gb = [turn_g(i + 1, 0), turn_g(i + 1, 1)]
+                    if not CFG["lp%d" % i] and (i or not CFG["early"]):
                         load_p(i + 1, 0, gb[0])
                         load_p(i + 1, 1, gb[1])
                 else:
@@ -352,7 +364,7 @@ def tile_weightedsignedseminmfupdate_x1_kernel(tc, x, f, w, g, p, q, out, words,
             for nm, v in onv:
                 relu_v(i, 2 * c + v, nm)
             merge(i, 2 * c + 1)
-            if i + 1 < GROUPS and c == 0 and CFG["lp%d" % i]:
+            if i + 1 < GROUPS and c == 0 and CFG["lp%d" % i] and (i or not CFG["early"]):
                 load_p(i + 1, 0, gb[0])
                 load_p(i + 1, 1, gb[1])
             nxt = 2 * s + 2
@@ -362,7 +374,7 @@ def tile_weightedsignedseminmfupdate_x1_kernel(tc, x, f, w, g, p, q, out, words,
         parts = [slice(0, 256), slice(256, 384), slice(384, 512)]
         root(i, four, "num")
         ratio(i - 1, lo)
-        update(i - 1, lo, nc.gpsimd)
+        update(i - 1, lo, nc.gpsimd if CFG["g2"] else nc.vector)
         store_out(i - 1, lo)
         if CFG["r1"] == "V":
             lay_r(i - 2, every, "V")

CFG = {"f0":"S","f1":"S","x00":"S","x01":"S","x10":"S","x11":"G","x20":"S","x21":"G","x30":"S","x31":"G","e11":1,"r0":"V","r1":"V","r2":"S","t0":"S","t1":"S","gt":0,"g3":0,"sc":"S","qx":2,"lp0":1,"lp1":0,"lp2":0,"vr0":0,"vr1":0,"vr2":0,"vr3":1,"vr4":1,"vr5":1,"vr6":1,"vr7":1,"g2":0,"early":1}
NLAY = 6
from contextlib import ExitStack

import concourse.mybir as mybir
from concourse.masks import make_identity

M, N, R = 1024, 2048, 512
FLOPS = 2 * M * N * R + 2 * M * R * R + 2 * N * R * R

F32 = mybir.dt.float32
BF16 = mybir.dt.bfloat16
I32 = mybir.dt.int32
U32 = mybir.dt.uint32
U8 = mybir.dt.uint8
FP8X4 = mybir.dt.float8_e4m3fn_x4
ALU = mybir.AluOpType
ACT = mybir.ActivationFunctionType

P = 128
PACK = 4
ROWS = P * PACK
HALVES = M // ROWS
GROUPS = N // ROWS
OFFSET = 0.5


def tile_weightedsignedseminmfupdate_x1_kernel(tc, x, f, w, g, p, q, out, words, scales):
    nc = tc.nc
    with ExitStack() as ctx:
        keep = ctx.enter_context(tc.tile_pool(name="keep", bufs=1))
        work = ctx.enter_context(tc.tile_pool(name="work", bufs=2))
        psum = ctx.enter_context(tc.psum_pool(name="psum", bufs=2))

        def kept(shape, dtype, name):
            return keep.tile(shape, dtype, name=name, align_bytes=64)

        def temp(shape, dtype, name, bufs=2):
            return work.tile(shape, dtype, name=name, bufs=bufs, align_bytes=64)

        p_col = kept([P, PACK], BF16, "p_col")
        q_col = kept([P, PACK], BF16, "q_col")
        w_col = kept([P, HALVES, PACK], BF16, "w_col")
        f_raw = [kept([P, PACK, R], BF16, "f_raw%d" % h) for h in range(HALVES)]
        g_raw = [kept([P, PACK, R], BF16, "g_raw%d" % i) for i in range(GROUPS)]
        x_raw = [[kept([P, PACK, ROWS], BF16, "x_raw%d%d" % (i, h)) for h in range(HALVES)] for i in range(GROUPS)]

        def load_f(h):
            nc.sync.dma_start(out=f_raw[h][:], in_=f[h * ROWS:(h + 1) * ROWS, :].rearrange("(k j) r -> k j r", j=PACK))

        def load_g(i):
            nc.sync.dma_start(out=g_raw[i][:], in_=g[i * ROWS:(i + 1) * ROWS, :].rearrange("(m t) r -> m t r", t=PACK))

        def load_x(i, h):
            nc.sync.dma_start(
                out=x_raw[i][h][:],
                in_=x[h * ROWS:(h + 1) * ROWS, i * ROWS:(i + 1) * ROWS].rearrange("(k j) n -> k j n", j=PACK),
            )

        ident_b = kept([P, P], BF16, "ident_b")
        ident_f = kept([P, P], F32, "ident_f")
        make_identity(nc, ident_b[:])
        make_identity(nc, ident_f[:])

        ctx.enter_context(tc.manual_schedule())

        nc.sync.dma_start(out=p_col[:], in_=p.rearrange("(k t) -> k t", t=PACK))
        if CFG["x00"] == "V0":
            load_x(0, 0)
        load_f(0)
        load_f(1)
        load_g(0)
        nc.sync.dma_start(out=w_col[:], in_=w.rearrange("(h k j) -> k h j", h=HALVES, j=PACK))
        if CFG["x00"] != "V0":
            load_x(0, 0)
        load_x(0, 1)
        nc.sync.dma_start(out=q_col[:], in_=q.rearrange("(k t) -> k t", t=PACK))
        for i in range(1, GROUPS):
            load_g(i)
            load_x(i, 0)
            load_x(i, 1)

        def pair(width, name):
            return kept([P, width], U32, name + "_codes"), kept([P, width], U8, name + "_scales")

        f_q = [pair(R, "fq%d" % h) for h in range(HALVES)]
        fw_q = [pair(R, "fwq%d" % h) for h in range(HALVES)]
        b_q = pair(R, "bq")
        x_q = [[pair(ROWS, "xq%d%d" % (i, h)) for h in range(HALVES)] for i in range(GROUPS)]
        g_q = [pair(ROWS, "gq%d" % i) for i in range(GROUPS)]

        def quantize(dst, cols, values):
            nc.vector.quantize_mx(out=dst[0][:, cols].bitcast(FP8X4), scales=dst[1][:, cols], in_=values)

        def multiply(acc, left, left_cols, right, right_cols, start, stop):
            nc.tensor.matmul_mx(
                out=acc,
                lhsT=left[0][:, left_cols].bitcast(FP8X4),
                lhsT_scale=left[1][:, left_cols],
                rhs=right[0][:, right_cols].bitcast(FP8X4),
                rhs_scale=right[1][:, right_cols],
                start=start,
                stop=stop,
            )

        every = slice(0, R)

        def tile_cols(t):
            return slice(t * P, (t + 1) * P)

        warm = kept([P, 1], F32, "warm")
        nc.gpsimd.memset(warm[:], 1.0)
        nc.scalar.activation(out=warm[:], in_=warm[:], func=ACT.Abs_reciprocal_sqrt)

        s_two = kept([P, PACK], F32, "s_two")
        s_col = kept([P, PACK], BF16, "s_col")
        qs_col = kept([P, PACK], F32, "qs_col")
        s_row = kept([P, R], BF16, "s_row")
        nc.vector.tensor_scalar(out=s_two[:], in0=p_col[:], scalar1=0.0, scalar2=2.0, op0=ALU.is_ge, op1=ALU.mult)
        nc.vector.tensor_scalar(out=s_col[:], in0=s_two[:], scalar1=1.0, scalar2=None, op0=ALU.subtract)
        s_bank = psum.tile([P, 2 * R], BF16, name="bank", bufs=8)
        for t in range(PACK):
            nc.tensor.transpose(out=s_bank[:, tile_cols(t)], in_=s_col[:, t:t + 1].to_broadcast([P, P]), identity=ident_b[:])
        s_out, s_in = s_row[:].rearrange("p (m t) -> p m t", t=PACK), s_bank[:, 0:R].rearrange("p (t m) -> p m t", t=PACK)
        if CFG["sc"] == "S":
            nc.scalar.copy(out=s_out, in_=s_in)
        else:
            nc.vector.tensor_copy(out=s_out, in_=s_in)

        fs = f_raw
        f_il = [temp([P, R, PACK], BF16, "lay", bufs=NLAY) for h in range(HALVES)]
        fw_il = [temp([P, R, PACK], BF16, "lay", bufs=NLAY) for h in range(HALVES)]

        def sign_f(h):
            nc.vector.tensor_tensor(out=fs[h][:], in0=f_raw[h][:], in1=s_row[:].unsqueeze(1).to_broadcast([P, PACK, R]), op=ALU.mult)

        def interleave(engine, dst, src):
            if engine == "V":
                nc.vector.tensor_copy(
                    out=dst[:].rearrange("p (t b c) j -> p b t (c j)", t=PACK, c=2).rearrange("p b t (c j) -> p b t c j", c=2) if not CFG.get("v3") else dst[:].rearrange("p (t m) j -> p m t j", t=PACK),
                    in_=src[:].rearrange("p j (b c t) -> p b t c j", t=PACK, c=2) if not CFG.get("v3") else src[:].rearrange("p j (m t) -> p m t j", t=PACK))
            else:
                nc.scalar.copy(
                    out=dst[:].rearrange("p (t m) j -> p m t j", t=PACK),
                    in_=src[:].rearrange("p j (m t) -> p m t j", t=PACK))

        def weigh_f(h):
            nc.vector.tensor_tensor(out=fw_il[h][:], in0=f_il[h][:], in1=w_col[:, h, :].unsqueeze(1).to_broadcast([P, R, PACK]), op=ALU.mult)

        def flat(t):
            return t[:].rearrange("p c j -> p (c j)")

        def gram(c):
            bank = psum.tile([P, PACK, P], F32, name="bank", bufs=8)
            for t in range(PACK):
                for h in range(HALVES):
                    multiply(bank[:, t, :], f_q[h], tile_cols(t), fw_q[h], tile_cols(c), h == 0, h == HALVES - 1)
            return bank

        b_il = temp([P, R, PACK], BF16, "lay", bufs=NLAY)

        def gain_b(c, bank):
            nc.vector.tensor_tensor(out=b_il[:, tile_cols(c), :], in0=bank[:].rearrange("p t r -> p r t"), in1=qs_col[:].unsqueeze(1).to_broadcast([P, P, PACK]), op=ALU.mult)

        def quant_b(c):
            quantize(b_q, tile_cols(c), b_il[:, tile_cols(c), :].rearrange("p c j -> p (c j)"))

        g_il = {}

        def turn_g(i, pair_):
            bank = psum.tile([P, 2 * 2 * P], F32, name="bank", bufs=8)
            for u in range(2):
                for v in range(2):
                    t = 2 * pair_ + v
                    at = (2 * u + v) * P
                    nc.tensor.transpose(out=bank[:, at:at + P], in_=g_raw[i][:, t, :].bitcast(F32)[:, u:2 * P:2], identity=ident_f[:])
            return bank

        def load_p(i, pair_, bank):
            if i not in g_il:
                g_il[i] = temp([P, ROWS, PACK], BF16, "lay", bufs=NLAY)
            nc.vector.tensor_tensor(
                out=g_il[i][:, pair_ * 2 * P:(pair_ + 1) * 2 * P, :].rearrange("p n (u e) -> p n u e", u=2),
                in0=bank[:].bitcast(BF16).rearrange("p (u n e) -> p n u e", u=2, e=2),
                in1=p_col[:].rearrange("p (u e) -> p u e", u=2).unsqueeze(1).to_broadcast([P, 2 * P, 2, 2]),
                op=ALU.mult,
            )

        def quant_g(i):
            quantize(g_q[i], every, flat(g_il[i]))

        x_il = {}

        def lay_x(i, h, engine):
            slot = "lay" if (i, h) == (0, 1) else ("x_even", "x_odd")[h]
            x_il[i, h] = temp([P, ROWS, PACK], BF16, slot, bufs=NLAY if slot == "lay" else 1)
            if engine == "G":
                nc.gpsimd.tensor_scalar(
                    out=x_il[i, h][:].rearrange("p (t m) j -> p m t j", t=PACK),
                    in0=x_raw[i][h][:].rearrange("p j (m t) -> p m t j", t=PACK),
                    scalar1=1.0, scalar2=0.0, op0=ALU.mult, op1=ALU.add)
                return
            interleave(engine, x_il[i, h], x_raw[i][h])

        def quant_x(i, h):
            quantize(x_q[i][h], every, flat(x_il[i, h]))

        a_bank, c_bank, ra, rc = {}, {}, {}, {}
        num, den, y_den, y_num, res = {}, {}, {}, {}, {}

        def mm(i, ts):
            for t in ts:
                a_bank[i, t] = psum.tile([P, R], F32, name="bank", bufs=8)
                for h in range(HALVES):
                    multiply(a_bank[i, t][:], x_q[i][h], tile_cols(t), fw_q[h], every, h == 0, h == HALVES - 1)
            for t in ts:
                c_bank[i, t] = psum.tile([P, R], F32, name="bank", bufs=8)
                multiply(c_bank[i, t][:], g_q[i], tile_cols(t), b_q, every, True, True)

        def natural(bank):
            return bank[:].rearrange("p (t m) -> p m t", t=PACK)

        def by_four(tile_):
            return tile_[:].rearrange("p (m t) -> p m t", t=PACK)

        def relu(i, ts, on_vector=()):
            for part, bank, nm in ((ra, a_bank, "ra"), (rc, c_bank, "rc")):
                for t in ts:
                    part[i, t] = temp([P, R], F32, nm, bufs=4)
                    if (nm, t % 2) not in on_vector:
                        nc.scalar.activation(out=by_four(part[i, t]), in_=natural(bank[i, t]), func=ACT.Relu, scale=-1.0)

        def relu_v(i, t, nm):
            part, bank = (ra, a_bank) if nm == "ra" else (rc, c_bank)
            nc.vector.tensor_scalar(out=by_four(part[i, t]), in0=natural(bank[i, t]), scalar1=0.0, scalar2=-1.0, op0=ALU.min, op1=ALU.mult)

        def merge(i, t, first="num"):
            if i not in num:
                num[i] = temp([P, PACK, R], F32, "num", bufs=3)
                den[i] = temp([P, PACK, R], F32, "den", bufs=3)
            for dst, bank, part in ((num[i], a_bank[i, t], rc[i, t]), (den[i], c_bank[i, t], ra[i, t])):
                nc.vector.scalar_tensor_tensor(
                    out=dst[:, t, :].rearrange("p (m t) -> p m t", t=PACK), in0=natural(bank), scalar=0.0,
                    in1=by_four(part), op0=ALU.max, op1=ALU.add)

        def root(i, ts, which, cols=slice(0, R)):
            src, func = (num, ACT.Sqrt) if which == "num" else (den, ACT.Abs_reciprocal_sqrt)
            nc.scalar.activation(out=src[i][:, ts, cols], in_=src[i][:, ts, cols], func=func, bias=OFFSET)

        def ratio(i, ts, cols=slice(0, R)):
            nc.vector.tensor_tensor(out=num[i][:, ts, cols], in0=num[i][:, ts, cols], in1=den[i][:, ts, cols], op=ALU.mult)

        def update(i, ts, engine=nc.vector, cols=slice(0, R)):
            if i not in res:
                res[i] = temp([P, PACK, R], F32, "res")
            engine.tensor_tensor(out=res[i][:, ts, cols], in0=num[i][:, ts, cols], in1=g_raw[i][:, ts, cols], op=ALU.mult)

        def store_out(i, ts, cols=slice(0, R)):
            nc.sync.dma_start(out=out[i * ROWS:(i + 1) * ROWS, :].rearrange("(m t) r -> m t r", t=PACK)[:, ts, cols], in_=res[i][:, ts, cols])

        r_il, r_codes = {}, {}
        r_scales = kept([P, GROUPS, R], U8, "r_scales")

        def lay_r(i, cols, engine="V"):
            if i not in r_il:
                r_il[i] = temp([P, R, PACK], BF16, "r_il")
                r_codes[i] = temp([P, R], U32, "r_codes")
            o = r_il[i][:, cols, :].rearrange("p (c i) t -> p c t i", i=PACK)
            s = res[i][:, :, cols].rearrange("p t (c i) -> p c t i", i=PACK)
            if engine == "V":
                nc.vector.tensor_copy(out=o, in_=s)
            else:
                nc.scalar.copy(out=o, in_=s)

        def quant_r(i, cols):
            nc.vector.quantize_mx(out=r_codes[i][:, cols].bitcast(FP8X4), scales=r_scales[:, i, cols], in_=r_il[i][:, cols, :].rearrange("p c j -> p (c j)"))

        def store_words(i, cols):
            nc.sync.dma_start(out=words.rearrange("g k m t -> g k (m t)")[i, :, :].bitcast(I32)[:, cols], in_=r_codes[i][:, cols].bitcast(I32))

        def store_scales(i):
            for Q in range(4):
                nc.sync.dma_start(out=scales[i, 4 * Q:4 * Q + 4, :].bitcast(I32), in_=r_scales[32 * Q:32 * Q + 4, i, :].bitcast(I32))

        def store_planes(i):
            store_words(i, every)
            store_scales(i)

        lo, hi, four = slice(0, 2), slice(2, 4), slice(0, 4)
        right = slice(R // 2, R)
        gb = [turn_g(0, 0), turn_g(0, 1)]
        if CFG["x00"] == "V0":
            lay_x(0, 0, "V")
        sign_f(0)
        interleave(CFG["f0"], f_il[0], fs[0])
        sign_f(1)
        interleave(CFG["f1"], f_il[1], fs[1])
        load_p(0, 0, gb[0])
        load_p(0, 1, gb[1])
        if CFG["x00"] != "V0":
            lay_x(0, 0, CFG["x00"])
        weigh_f(0)
        quant_g(0)
        quantize(f_q[0], every, flat(f_il[0]))
        quantize(fw_q[0], every, flat(fw_il[0]))
        weigh_f(1)
        quantize(f_q[1], every, flat(f_il[1]))
        quantize(fw_q[1], every, flat(fw_il[1]))
        lay_x(0, 1, CFG["x01"])
        if CFG["early"]:
            gb = [turn_g(1, 0), turn_g(1, 1)]
        banks = [gram(c) for c in range(4)]
        quant_x(0, 0)
        nc.vector.tensor_tensor(out=qs_col[:], in0=s_col[:], in1=q_col[:], op=ALU.mult)
        if CFG["x11"] == "G":
            lay_x(1, 1, "G")
        if CFG["early"]:
            load_p(1, 0, gb[0])
            load_p(1, 1, gb[1])
        for c in range(4):
            gain_b(c, banks[c])
            if c == CFG["qx"]:
                quant_x(0, 1)
        quantize(b_q, every, flat(b_il))
        lay_x(1, 0, CFG["x10"])

        mm(0, (0, 1))
        VR = [CFG["vr%d" % s] for s in range(8)]
        if CFG["x11"] != "G" and CFG["e11"]:
            lay_x(1, 1, CFG["x11"])
        for s in range(2 * GROUPS):
            i, c = divmod(s, 2)
            pair_ = (2 * c, 2 * c + 1)
            onv = [(nm, 1) for nm in ("ra", "rc")[:VR[s]]]
            relu(i, pair_, onv)
            if i >= 3 and c == 0:
                lay_r(i - 3, every, CFG["r0"])
            if i >= 3 and c == 1:
                quant_r(i - 3, every)
                store_planes(i - 3)
            if i + 1 < GROUPS:
                if c == 0:
                    if i == 0 and CFG["x11"] != "G" and not CFG["e11"]:
                        lay_x(1, 1, CFG["x11"])
                    if i or not CFG["early"]:
                        gb = [turn_g(i + 1, 0), turn_g(i + 1, 1)]
                    if not CFG["lp%d" % i] and (i or not CFG["early"]):
                        load_p(i + 1, 0, gb[0])
                        load_p(i + 1, 1, gb[1])
                else:
                    quant_g(i + 1)
                quant_x(i + 1, c)
            if i >= 1:
                order = ("den", "num") if i % 2 else ("num", "den")
                root(i - 1, four, order[c])
            if i + 2 < GROUPS:
                lay_x(i + 2, c, CFG["x%d%d" % (i + 2, c)])
            if i >= 2:
                half = (lo, hi)[c]
                ratio(i - 2, half)
                update(i - 2, half, nc.gpsimd)
                store_out(i - 2, half)
            merge(i, 2 * c)
            for nm, v in onv:
                relu_v(i, 2 * c + v, nm)
            merge(i, 2 * c + 1)
            if i + 1 < GROUPS and c == 0 and CFG["lp%d" % i] and (i or not CFG["early"]):
                load_p(i + 1, 0, gb[0])
                load_p(i + 1, 1, gb[1])
            nxt = 2 * s + 2
            if nxt < GROUPS * PACK:
                mm(nxt // PACK, (nxt % PACK, nxt % PACK + 1))
        i = GROUPS - 1
        parts = [slice(0, 256), slice(256, 384), slice(384, 512)]
        root(i, four, "num")
        ratio(i - 1, lo)
        update(i - 1, lo, nc.gpsimd if CFG["g2"] else nc.vector)
        store_out(i - 1, lo)
        if CFG["r1"] == "V":
            lay_r(i - 2, every, "V")
        ratio(i - 1, hi)
        update(i - 1, hi, nc.gpsimd if CFG["gt"] else nc.vector)
        store_out(i - 1, hi)
        for cols in parts:
            root(i, four, "den", cols)
        if CFG["r1"] == "S":
            lay_r(i - 2, every, "S")
        if CFG["r2"] == "V":
            lay_r(i - 1, every, "V")
        ratio(i, four, parts[0])
        quant_r(i - 2, every)
        store_planes(i - 2)
        if CFG["r2"] == "S":
            lay_r(i - 1, every, "S")
        update(i, four, nc.gpsimd if CFG["g3"] else nc.vector, parts[0])
        store_out(i, four, parts[0])
        ratio(i, four, parts[1])
        if CFG["r2"] == "V":
            quant_r(i - 1, every)
            store_planes(i - 1)
        update(i, four, nc.vector, parts[1])
        if CFG["t0"] == "V":
            lay_r(i, parts[0], "V")
        ratio(i, four, parts[2])
        if CFG["t0"] == "S":
            lay_r(i, parts[0], "S")
        if CFG["r2"] == "S":
            quant_r(i - 1, every)
            store_planes(i - 1)
        lay_r(i, parts[1], CFG["t1"])
        update(i, four, nc.vector, parts[2])
        store_out(i, four, right)
        quant_r(i, parts[0])
        store_words(i, parts[0])
        lay_r(i, parts[2], "V")
        quant_r(i, parts[1])
        quant_r(i, parts[2])
        store_words(i, right)
        store_scales(i)
